import numpy as np
import ml_dtypes


def mxq(x, axis, fmt="e4m3"):
    dtype, down = {"e4m3": (ml_dtypes.float8_e4m3fn, 7), "e5m2": (ml_dtypes.float8_e5m2, 14)}[fmt]
    v = np.moveaxis(np.asarray(x, np.float32).astype(ml_dtypes.bfloat16).astype(np.float64), axis, -1)
    blocks = v.reshape(v.shape[:-1] + (-1, 32))
    amax = np.abs(blocks).max(-1, keepdims=True)
    byte = np.maximum(np.where(amax > 0, np.frexp(amax)[1] - 1 + 127, 0) - down, 1)
    scale = np.exp2(byte - 127.0)
    codes = (blocks / scale).astype(np.float32).astype(dtype).astype(np.float64)
    return np.moveaxis((codes * scale).reshape(v.shape), -1, axis)


WIDE = False


def mx_kscale(k):
    if not WIDE:
        return np.ones(k)
    levels = np.array([10, -10, 5, -5, 0])
    if k % 512:
        return np.exp2(np.random.permutation(np.resize(levels, k // 32))).repeat(32)
    a = np.empty((k // 512, 16))
    for p in range(k // 512):
        a[p, :8] = np.random.permutation(np.resize(levels, 8))
        for g in range(8):
            far = levels[np.abs(levels - a[p, g]) >= 10]
            a[p, g + 8] = far[np.random.randint(len(far))]
    return np.exp2(a.ravel()).repeat(32)


def f64(x):
    return np.asarray(x).astype(np.float64)


def striped(idx):
    return np.tile(idx.reshape(-1, 16).T, (8, 1)).astype(np.uint16)


def unstriped(offs):
    return offs[:16].T.reshape(-1).astype(np.int64)


K, T, D, S, V, N = 2048, 512, 2, 512, 256, 128


def setup_inputs():
    n = np.random.standard_normal
    s = mx_kscale(K)[:, None]
    return {
        "xT": (n((K, T)) * s).astype(np.float32),
        "w": (n((D, K, N)) / np.sqrt(D * K) / s[None]).astype(np.float32),
        "offs": striped(np.random.permutation(T)[:S]),
    }


def reference(xT, w, offs):
    idx = unstriped(offs)
    xq = mxq(f64(xT)[:, idx], 0, "e4m3")
    wq = mxq(f64(w), 1, "e4m3")
    y = sum(wq[d].T @ xq[:, d * V:(d + 1) * V] for d in range(D))
    return y

@@ -1,0 +1,140 @@
+from contextlib import ExitStack
+
+import concourse.mybir as mybir
+
+K, T, D, V, N = 2048, 512, 2, 256, 128
+FLOPS = 2 * D * K * V * N
+
+F32 = mybir.dt.float32
+BF16 = mybir.dt.bfloat16
+U32 = mybir.dt.uint32
+U16 = mybir.dt.uint16
+U8 = mybir.dt.uint8
+FP8X4 = mybir.dt.float8_e4m3fn_x4
+COPY = mybir.ActivationFunctionType.Copy
+
+P = 128
+PACK = 4
+K_PASS = P * PACK
+PASSES = K // K_PASS
+RUN = 2
+LIST_COLS = V // 16
+HALF = T // 2
+VECTOR_TOKENS = (256, 112, 112, 192)
+
+
+def interleave_views(grouped, raw, cols):
+    dst = grouped[:, cols, :].rearrange("p (c i) j -> p c j i", i=RUN)
+    src = raw[:, :, cols].rearrange("p j (c i) -> p c j i", i=RUN)
+    return dst, src
+
+
+def tile_picked_merge_lin_none_sub_e_kernel(tc, xT, w, offs, out):
+    nc = tc.nc
+
+    def copy_scalar(grouped, raw, cols):
+        dst, src = interleave_views(grouped, raw, cols)
+        nc.scalar.activation(out=dst, in_=src, func=COPY)
+
+    def copy_vector(grouped, raw, cols):
+        dst, src = interleave_views(grouped, raw, cols)
+        nc.vector.tensor_copy(out=dst, in_=src)
+
+    with ExitStack() as ctx:
+        keep = ctx.enter_context(tc.tile_pool(name="keep", bufs=1))
+        psum = ctx.enter_context(tc.psum_pool(name="psum", bufs=1))
+
+        offsets = keep.tile([P, D * LIST_COLS], U16, name="offsets")
+        x_raw = [keep.tile([P, PACK, T], F32, name=f"x_raw{a}", align_bytes=64) for a in range(PASSES)]
+        x_bf = [keep.tile([P, T, PACK], BF16, name=f"x_bf{a}", align_bytes=64) for a in range(PASSES)]
+        x_words = [keep.tile([P, T], U32, name=f"x_words{a}", align_bytes=64) for a in range(PASSES)]
+        x_scales = keep.tile([P, T], U8, name="x_scales", align_bytes=64)
+        units = [(d, a) for d in range(D) for a in range(PASSES)]
+        g_words = {u: keep.tile([P, V], U32, name=f"g_words{u[0]}_{u[1]}", align_bytes=64) for u in units}
+        g_scales = [keep.tile([P, V], U8, name=f"g_scales{d}", align_bytes=64) for d in range(D)]
+        w_raw = {u: keep.tile([P, PACK, N], F32, name=f"w_raw{u[0]}_{u[1]}", align_bytes=64) for u in units}
+        w_bf = {u: keep.tile([P, N, PACK], BF16, name=f"w_bf{u[0]}_{u[1]}", align_bytes=64) for u in units}
+        w_words = {u: keep.tile([P, N], U32, name=f"w_words{u[0]}_{u[1]}", align_bytes=64) for u in units}
+        w_scales = {u: keep.tile([P, N], U8, name=f"w_scales{u[0]}_{u[1]}", align_bytes=64) for u in units}
+        warm_in = keep.tile([P, 2], F32, name="warm_in")
+        warm_out = keep.tile([P, 2], BF16, name="warm_out")
+        result = keep.tile([N, V], F32, name="result")
+        acc = psum.tile([N, V], F32, name="acc")
+
+        def rows(a):
+            return slice(a * K_PASS, (a + 1) * K_PASS)
+
+        for a in range(PASSES):
+            nc.sync.dma_start(out=x_raw[a][:], in_=xT[rows(a), :].rearrange("(p j) t -> p j t", j=PACK))
+            if a == 0:
+                nc.sync.dma_start(offsets[:], offs)
+        for d, a in units:
+            nc.sync.dma_start(out=w_raw[d, a][:], in_=w[d, rows(a), :].rearrange("(p j) n -> p j n", j=PACK))
+
+        nc.vector.memset(warm_in[:], 0.0)
+        nc.scalar.activation(out=warm_out[:], in_=warm_in[:], func=COPY)
+        nc.gpsimd.memset(x_scales[:], 0)
+
+        def quantize_x(a, cols):
+            nc.vector.quantize_mx(
+                out=x_words[a][:, cols].bitcast(FP8X4),
+                scales=x_scales[PACK * a :, cols],
+                in_=x_bf[a][:, cols, :].rearrange("p t j -> p (t j)"),
+            )
+
+        def piece(d):
+            return offsets[:, d * LIST_COLS : (d + 1) * LIST_COLS]
+
+        def gather_words(d, a):
+            nc.vector.tensor_copy(out=g_words[d, a][:], in_=x_words[a][:].indirect(piece(d)))
+
+        def gather_scales(d):
+            nc.vector.tensor_copy(out=g_scales[d][:], in_=x_scales[:].indirect(piece(d)))
+
+        def quantize_w(u):
+            nc.vector.quantize_mx(
+                out=w_words[u][:].bitcast(FP8X4),
+                scales=w_scales[u][:],
+                in_=w_bf[u][:].rearrange("p n j -> p (n j)"),
+            )
+
+        def multiply(u):
+            d, a = u
+            nc.tensor.matmul_mx(
+                out=acc[:],
+                lhsT=w_words[u][:].bitcast(FP8X4),
+                lhsT_scale=w_scales[u][:],
+                rhs=g_words[u][:].bitcast(FP8X4),
+                rhs_scale=g_scales[d][PACK * a :, :],
+                start=(u == units[0]),
+                stop=(u == units[-1]),
+            )
+
+        low, high = slice(0, HALF), slice(HALF, T)
+        for a in range(PASSES):
+            copy_scalar(x_bf[a], x_raw[a], low)
+            cut = T - VECTOR_TOKENS[a]
+            if cut > HALF:
+                copy_scalar(x_bf[a], x_raw[a], slice(HALF, cut))
+            copy_vector(x_bf[a], x_raw[a], slice(cut, T))
+            quantize_x(a, low)
+            quantize_x(a, high)
+            if a < PASSES - 1:
+                for d in range(D):
+                    gather_words(d, a)
+
+        for d in range(D):
+            gather_words(d, PASSES - 1)
+            gather_scales(d)
+            for a in range(PASSES):
+                u = (d, a)
+                if u == units[-1]:
+                    copy_scalar(w_bf[u], w_raw[u], slice(0, 48))
+                    copy_vector(w_bf[u], w_raw[u], slice(48, N))
+                else:
+                    copy_scalar(w_bf[u], w_raw[u], slice(0, N))
+                quantize_w(u)
+                multiply(u)
+
+        nc.vector.tensor_copy(out=result[:], in_=acc[:])
+        nc.sync.dma_start(out=out, in_=result[:])

@@ -20,7 +20,9 @@ PASSES = K // K_PASS
 RUN = 2
 LIST_COLS = V // 16
 HALF = T // 2
-VECTOR_TOKENS = (256, 112, 112, 192)
+VECTOR_TOKENS = ((128, 128), (0, 80), (0, 80), (0, 128))
+W_GROUPS = ((0, 2), (2, 4), (4, 6), (6, 7), (7, 8))
+VECTOR_W_COLS = {6: 32, 7: 80}
 
 
 def interleave_views(grouped, raw, cols):
@@ -45,17 +47,19 @@ def tile_picked_merge_lin_none_sub_e_kernel(tc, xT, w, offs, out):
         psum = ctx.enter_context(tc.psum_pool(name="psum", bufs=1))
 
         offsets = keep.tile([P, D * LIST_COLS], U16, name="offsets")
-        x_raw = [keep.tile([P, PACK, T], F32, name=f"x_raw{a}", align_bytes=64) for a in range(PASSES)]
-        x_bf = [keep.tile([P, T, PACK], BF16, name=f"x_bf{a}", align_bytes=64) for a in range(PASSES)]
+        halves = [(a, h) for a in range(PASSES) for h in range(2)]
+        x_raw = {u: keep.tile([P, PACK, HALF], F32, name=f"x_raw{u[0]}_{u[1]}", align_bytes=64) for u in halves}
+        x_bf = {u: keep.tile([P, HALF, PACK], BF16, name=f"x_bf{u[0]}_{u[1]}", align_bytes=64) for u in halves}
         x_words = [keep.tile([P, T], U32, name=f"x_words{a}", align_bytes=64) for a in range(PASSES)]
         x_scales = keep.tile([P, T], U8, name="x_scales", align_bytes=64)
-        units = [(d, a) for d in range(D) for a in range(PASSES)]
+        last = PASSES - 1
+        units = [(d, a) for d in range(D) for a in range(last)] + [(d, last) for d in range(D)]
         g_words = {u: keep.tile([P, V], U32, name=f"g_words{u[0]}_{u[1]}", align_bytes=64) for u in units}
         g_scales = [keep.tile([P, V], U8, name=f"g_scales{d}", align_bytes=64) for d in range(D)]
         w_raw = {u: keep.tile([P, PACK, N], F32, name=f"w_raw{u[0]}_{u[1]}", align_bytes=64) for u in units}
-        w_bf = {u: keep.tile([P, N, PACK], BF16, name=f"w_bf{u[0]}_{u[1]}", align_bytes=64) for u in units}
-        w_words = {u: keep.tile([P, N], U32, name=f"w_words{u[0]}_{u[1]}", align_bytes=64) for u in units}
-        w_scales = {u: keep.tile([P, N], U8, name=f"w_scales{u[0]}_{u[1]}", align_bytes=64) for u in units}
+        w_bf = keep.tile([P, len(units), N, PACK], BF16, name="w_bf", align_bytes=64)
+        w_words = keep.tile([P, len(units), N], U32, name="w_words", align_bytes=64)
+        w_scales = keep.tile([P, len(units), N], U8, name="w_scales", align_bytes=64)
         warm_in = keep.tile([P, 2], F32, name="warm_in")
         warm_out = keep.tile([P, 2], BF16, name="warm_out")
         result = keep.tile([N, V], F32, name="result")
@@ -64,9 +68,12 @@ def tile_picked_merge_lin_none_sub_e_kernel(tc, xT, w, offs, out):
         def rows(a):
             return slice(a * K_PASS, (a + 1) * K_PASS)
 
-        for a in range(PASSES):
-            nc.sync.dma_start(out=x_raw[a][:], in_=xT[rows(a), :].rearrange("(p j) t -> p j t", j=PACK))
-            if a == 0:
+        def tokens(h):
+            return slice(h * HALF, (h + 1) * HALF)
+
+        for a, h in halves:
+            nc.sync.dma_start(out=x_raw[a, h][:], in_=xT[rows(a), tokens(h)].rearrange("(p j) t -> p j t", j=PACK))
+            if (a, h) == halves[0]:
                 nc.sync.dma_start(offsets[:], offs)
         for d, a in units:
             nc.sync.dma_start(out=w_raw[d, a][:], in_=w[d, rows(a), :].rearrange("(p j) n -> p j n", j=PACK))
@@ -75,11 +82,11 @@ def tile_picked_merge_lin_none_sub_e_kernel(tc, xT, w, offs, out):
         nc.scalar.activation(out=warm_out[:], in_=warm_in[:], func=COPY)
         nc.gpsimd.memset(x_scales[:], 0)
 
-        def quantize_x(a, cols):
+        def quantize_x(a, h):
             nc.vector.quantize_mx(
-                out=x_words[a][:, cols].bitcast(FP8X4),
-                scales=x_scales[PACK * a :, cols],
-                in_=x_bf[a][:, cols, :].rearrange("p t j -> p (t j)"),
+                out=x_words[a][:, tokens(h)].bitcast(FP8X4),
+                scales=x_scales[PACK * a :, tokens(h)],
+                in_=x_bf[a, h][:].rearrange("p t j -> p (t j)"),
             )
 
         def piece(d):
@@ -91,50 +98,56 @@ def tile_picked_merge_lin_none_sub_e_kernel(tc, xT, w, offs, out):
         def gather_scales(d):
             nc.vector.tensor_copy(out=g_scales[d][:], in_=x_scales[:].indirect(piece(d)))
 
-        def quantize_w(u):
+        def quantize_w(i0, i1):
             nc.vector.quantize_mx(
-                out=w_words[u][:].bitcast(FP8X4),
-                scales=w_scales[u][:],
-                in_=w_bf[u][:].rearrange("p n j -> p (n j)"),
+                out=w_words[:, i0:i1, :].rearrange("p i n -> p (i n)").bitcast(FP8X4),
+                scales=w_scales[:, i0:i1, :].rearrange("p i n -> p (i n)"),
+                in_=w_bf[:, i0:i1, :, :].rearrange("p i n j -> p (i n j)"),
             )
 
-        def multiply(u):
+        def multiply(i):
+            u = units[i]
             d, a = u
             nc.tensor.matmul_mx(
                 out=acc[:],
-                lhsT=w_words[u][:].bitcast(FP8X4),
-                lhsT_scale=w_scales[u][:],
+                lhsT=w_words[:, i, :].bitcast(FP8X4),
+                lhsT_scale=w_scales[:, i, :],
                 rhs=g_words[u][:].bitcast(FP8X4),
                 rhs_scale=g_scales[d][PACK * a :, :],
                 start=(u == units[0]),
                 stop=(u == units[-1]),
             )
 
-        low, high = slice(0, HALF), slice(HALF, T)
+        def share_copy(grouped, raw, width, on_vector):
+            cut = width - on_vector
+            copy_scalar(grouped, raw, slice(0, cut))
+            if on_vector:
+                copy_vector(grouped, raw, slice(cut, width))
+
         for a in range(PASSES):
-            copy_scalar(x_bf[a], x_raw[a], low)
-            cut = T - VECTOR_TOKENS[a]
-            if cut > HALF:
-                copy_scalar(x_bf[a], x_raw[a], slice(HALF, cut))
-            copy_vector(x_bf[a], x_raw[a], slice(cut, T))
-            quantize_x(a, low)
-            quantize_x(a, high)
+            for h in range(2):
+                share_copy(x_bf[a, h], x_raw[a, h], HALF, VECTOR_TOKENS[a][h])
+                quantize_x(a, h)
             if a < PASSES - 1:
                 for d in range(D):
                     gather_words(d, a)
 
-        for d in range(D):
-            gather_words(d, PASSES - 1)
-            gather_scales(d)
-            for a in range(PASSES):
-                u = (d, a)
-                if u == units[-1]:
-                    copy_scalar(w_bf[u], w_raw[u], slice(0, 48))
-                    copy_vector(w_bf[u], w_raw[u], slice(48, N))
-                else:
-                    copy_scalar(w_bf[u], w_raw[u], slice(0, N))
-                quantize_w(u)
-                multiply(u)
+        def weights(i0, i1):
+            for i in range(i0, i1):
+                share_copy(w_bf[:, i, :, :], w_raw[units[i]], N, VECTOR_W_COLS.get(i, 0))
+            quantize_w(i0, i1)
+            for i in range(i0, i1):
+                multiply(i)
+
+        gather_scales(0)
+        weights(*W_GROUPS[0])
+        gather_scales(1)
+        weights(*W_GROUPS[1])
+        gather_words(0, last)
+        weights(*W_GROUPS[2])
+        gather_words(1, last)
+        weights(*W_GROUPS[3])
+        weights(*W_GROUPS[4])
 
         nc.vector.tensor_copy(out=result[:], in_=acc[:])
         nc.sync.dma_start(out=out, in_=result[:])

@@ -17,12 +17,18 @@ P = 128
 PACK = 4
 K_PASS = P * PACK
 PASSES = K // K_PASS
+LAST = PASSES - 1
 RUN = 2
 LIST_COLS = V // 16
 HALF = T // 2
-VECTOR_TOKENS = ((128, 128), (0, 80), (0, 80), (0, 128))
-W_GROUPS = ((0, 2), (2, 4), (4, 6), (6, 7), (7, 8))
-VECTOR_W_COLS = {6: 32, 7: 80}
+
+X_LOADS = (((0, 512),), ((0, 512),), ((0, 512),), ((0, 512),))
+X_SCALAR = (((0, 168),), ((0, 256), (256, 320)), ((0, 256), (256, 368)), ((0, 256),))
+X_VECTOR = (((168, 256), (256, 512)), ((320, 512),), ((368, 512),), ((256, 512),))
+X_QUANT = (((0, 256), (256, 512)), ((0, 256), (256, 512)), ((0, 256), (256, 512)), ((0, 256), (256, 512)))
+W_LOADS = ((0, 2), (2, 4), (4, 6), (6, 7), (7, 8))
+W_QUANT = ((0, 2), (2, 4), (4, 6), (6, 7), (7, 8))
+W_VECTOR_COLS = {}
 
 
 def interleave_views(grouped, raw, cols):
@@ -46,17 +52,26 @@ def tile_picked_merge_lin_none_sub_e_kernel(tc, xT, w, offs, out):
         keep = ctx.enter_context(tc.tile_pool(name="keep", bufs=1))
         psum = ctx.enter_context(tc.psum_pool(name="psum", bufs=1))
 
+        units = [(d, a) for d in range(D) for a in range(LAST)] + [(d, LAST) for d in range(D)]
+        loads = [(a, t0, t1) for a in range(PASSES) for t0, t1 in X_LOADS[a]]
+
         offsets = keep.tile([P, D * LIST_COLS], U16, name="offsets")
-        halves = [(a, h) for a in range(PASSES) for h in range(2)]
-        x_raw = {u: keep.tile([P, PACK, HALF], F32, name=f"x_raw{u[0]}_{u[1]}", align_bytes=64) for u in halves}
-        x_bf = {u: keep.tile([P, HALF, PACK], BF16, name=f"x_bf{u[0]}_{u[1]}", align_bytes=64) for u in halves}
+        x_raw = {
+            (a, t0): keep.tile([P, PACK, t1 - t0], F32, name=f"x_raw{a}_{t0}", align_bytes=64) for a, t0, t1 in loads
+        }
+        x_bf = [keep.tile([P, T, PACK], BF16, name=f"x_bf{a}", align_bytes=64) for a in range(PASSES)]
         x_words = [keep.tile([P, T], U32, name=f"x_words{a}", align_bytes=64) for a in range(PASSES)]
         x_scales = keep.tile([P, T], U8, name="x_scales", align_bytes=64)
-        last = PASSES - 1
-        units = [(d, a) for d in range(D) for a in range(last)] + [(d, last) for d in range(D)]
-        g_words = {u: keep.tile([P, V], U32, name=f"g_words{u[0]}_{u[1]}", align_bytes=64) for u in units}
-        g_scales = [keep.tile([P, V], U8, name=f"g_scales{d}", align_bytes=64) for d in range(D)]
-        w_raw = {u: keep.tile([P, PACK, N], F32, name=f"w_raw{u[0]}_{u[1]}", align_bytes=64) for u in units}
+        w_raw = {
+            i0: keep.tile([P, i1 - i0, PACK, N], F32, name=f"w_raw{i0}", tag=f"w_raw{i0}", align_bytes=64)
+            for i0, i1 in W_LOADS
+        }
+        g_words = {
+            (d, a): keep.tile([P, V], U32, name=f"g_words{d}_{a}", align_bytes=64) for d, a in units if a < LAST
+        }
+        g_scales = keep.tile([P, D, V], U8, name="g_scales", tag="w_raw0", align_bytes=64)
+        g_words[0, LAST] = keep.tile([P, V], U32, name="g_words_last0", tag="w_raw2", align_bytes=64)
+        g_words[1, LAST] = keep.tile([P, V], U32, name="g_words_last1", tag="w_raw4", align_bytes=64)
         w_bf = keep.tile([P, len(units), N, PACK], BF16, name="w_bf", align_bytes=64)
         w_words = keep.tile([P, len(units), N], U32, name="w_words", align_bytes=64)
         w_scales = keep.tile([P, len(units), N], U8, name="w_scales", align_bytes=64)
@@ -65,28 +80,35 @@ def tile_picked_merge_lin_none_sub_e_kernel(tc, xT, w, offs, out):
         result = keep.tile([N, V], F32, name="result")
         acc = psum.tile([N, V], F32, name="acc")
 
-        def rows(a):
-            return slice(a * K_PASS, (a + 1) * K_PASS)
+        w_passes = w.rearrange("d (a p j) n -> p (d a) (j n)", p=P, j=PACK)
 
-        def tokens(h):
-            return slice(h * HALF, (h + 1) * HALF)
-
-        for a, h in halves:
-            nc.sync.dma_start(out=x_raw[a, h][:], in_=xT[rows(a), tokens(h)].rearrange("(p j) t -> p j t", j=PACK))
-            if (a, h) == halves[0]:
+        for a, t0, t1 in loads:
+            rows = xT[a * K_PASS : (a + 1) * K_PASS, t0:t1]
+            nc.sync.dma_start(out=x_raw[a, t0][:], in_=rows.rearrange("(p j) t -> p j t", j=PACK))
+            if (a, t0) == (0, 0):
                 nc.sync.dma_start(offsets[:], offs)
-        for d, a in units:
-            nc.sync.dma_start(out=w_raw[d, a][:], in_=w[d, rows(a), :].rearrange("(p j) n -> p j n", j=PACK))
+        for i0, i1 in W_LOADS:
+            first = units[i0][0] * PASSES + units[i0][1]
+            final = units[i1 - 1][0] * PASSES + units[i1 - 1][1]
+            step = max(final - first, 1) // max(i1 - i0 - 1, 1)
+            nc.sync.dma_start(
+                out=w_raw[i0][:].rearrange("p i j n -> p i (j n)"),
+                in_=w_passes[:, first : final + 1 : step, :],
+            )
 
         nc.vector.memset(warm_in[:], 0.0)
         nc.scalar.activation(out=warm_out[:], in_=warm_in[:], func=COPY)
         nc.gpsimd.memset(x_scales[:], 0)
 
-        def quantize_x(a, h):
+        def copy_x(copy, a, t0, t1):
+            base = max(b for b, e in X_LOADS[a] if b <= t0)
+            copy(x_bf[a][:, base:, :], x_raw[a, base], slice(t0 - base, t1 - base))
+
+        def quantize_x(a, t0, t1):
             nc.vector.quantize_mx(
-                out=x_words[a][:, tokens(h)].bitcast(FP8X4),
-                scales=x_scales[PACK * a :, tokens(h)],
-                in_=x_bf[a, h][:].rearrange("p t j -> p (t j)"),
+                out=x_words[a][:, t0:t1].bitcast(FP8X4),
+                scales=x_scales[PACK * a :, t0:t1],
+                in_=x_bf[a][:, t0:t1, :].rearrange("p t j -> p (t j)"),
             )
 
         def piece(d):
@@ -96,58 +118,58 @@ def tile_picked_merge_lin_none_sub_e_kernel(tc, xT, w, offs, out):
             nc.vector.tensor_copy(out=g_words[d, a][:], in_=x_words[a][:].indirect(piece(d)))
 
         def gather_scales(d):
-            nc.vector.tensor_copy(out=g_scales[d][:], in_=x_scales[:].indirect(piece(d)))
+            nc.vector.tensor_copy(out=g_scales[:, d, :], in_=x_scales[:].indirect(piece(d)))
 
-        def quantize_w(i0, i1):
+        def weights(i0, i1):
+            for i in range(i0, i1):
+                cut = N - W_VECTOR_COLS.get(i, 0)
+                if cut > 0:
+                    copy_scalar(w_bf[:, i, :, :], w_raw[i0][:, i - i0, :, :], slice(0, cut))
+                if cut < N:
+                    copy_vector(w_bf[:, i, :, :], w_raw[i0][:, i - i0, :, :], slice(cut, N))
             nc.vector.quantize_mx(
                 out=w_words[:, i0:i1, :].rearrange("p i n -> p (i n)").bitcast(FP8X4),
                 scales=w_scales[:, i0:i1, :].rearrange("p i n -> p (i n)"),
                 in_=w_bf[:, i0:i1, :, :].rearrange("p i n j -> p (i n j)"),
             )
 
-        def multiply(i):
-            u = units[i]
-            d, a = u
-            nc.tensor.matmul_mx(
-                out=acc[:],
-                lhsT=w_words[:, i, :].bitcast(FP8X4),
-                lhsT_scale=w_scales[:, i, :],
-                rhs=g_words[u][:].bitcast(FP8X4),
-                rhs_scale=g_scales[d][PACK * a :, :],
-                start=(u == units[0]),
-                stop=(u == units[-1]),
-            )
-
-        def share_copy(grouped, raw, width, on_vector):
-            cut = width - on_vector
-            copy_scalar(grouped, raw, slice(0, cut))
-            if on_vector:
-                copy_vector(grouped, raw, slice(cut, width))
+        def multiply(i0, i1):
+            for i in range(i0, i1):
+                d, a = units[i]
+                nc.tensor.matmul_mx(
+                    out=acc[:],
+                    lhsT=w_words[:, i, :].bitcast(FP8X4),
+                    lhsT_scale=w_scales[:, i, :],
+                    rhs=g_words[d, a][:].bitcast(FP8X4),
+                    rhs_scale=g_scales[PACK * a :, d, :],
+                    start=(i == 0),
+                    stop=(i == len(units) - 1),
+                )
 
         for a in range(PASSES):
-            for h in range(2):
-                share_copy(x_bf[a, h], x_raw[a, h], HALF, VECTOR_TOKENS[a][h])
-                quantize_x(a, h)
-            if a < PASSES - 1:
+            for t0, t1 in X_SCALAR[a]:
+                copy_x(copy_scalar, a, t0, t1)
+            for t0, t1 in X_VECTOR[a]:
+                copy_x(copy_vector, a, t0, t1)
+            for t0, t1 in X_QUANT[a]:
+                quantize_x(a, t0, t1)
+            if a < LAST:
                 for d in range(D):
                     gather_words(d, a)
 
-        def weights(i0, i1):
-            for i in range(i0, i1):
-                share_copy(w_bf[:, i, :, :], w_raw[units[i]], N, VECTOR_W_COLS.get(i, 0))
-            quantize_w(i0, i1)
-            for i in range(i0, i1):
-                multiply(i)
-
+        weights(*W_QUANT[0])
         gather_scales(0)
-        weights(*W_GROUPS[0])
         gather_scales(1)
-        weights(*W_GROUPS[1])
-        gather_words(0, last)
-        weights(*W_GROUPS[2])
-        gather_words(1, last)
-        weights(*W_GROUPS[3])
-        weights(*W_GROUPS[4])
+        multiply(*W_QUANT[0])
+        weights(*W_QUANT[1])
+        gather_words(0, LAST)
+        multiply(*W_QUANT[1])
+        weights(*W_QUANT[2])
+        gather_words(1, LAST)
+        multiply(*W_QUANT[2])
+        for group in W_QUANT[3:]:
+            weights(*group)
+            multiply(*group)
 
         nc.vector.tensor_copy(out=result[:], in_=acc[:])
         nc.sync.dma_start(out=out, in_=result[:])

@@ -18,7 +18,7 @@ PACK = 4
 K_PASS = P * PACK
 PASSES = K // K_PASS
 LAST = PASSES - 1
-RUN = 2
+RUN = 4
 LIST_COLS = V // 16
 HALF = T // 2
 

from contextlib import ExitStack

import concourse.mybir as mybir

K, T, D, V, N = 2048, 512, 2, 256, 128
FLOPS = 2 * D * K * V * N

F32 = mybir.dt.float32
BF16 = mybir.dt.bfloat16
U32 = mybir.dt.uint32
U16 = mybir.dt.uint16
U8 = mybir.dt.uint8
FP8X4 = mybir.dt.float8_e4m3fn_x4
COPY = mybir.ActivationFunctionType.Copy

P = 128
PACK = 4
K_PASS = P * PACK
PASSES = K // K_PASS
LAST = PASSES - 1
RUN = 4
LIST_COLS = V // 16
HALF = T // 2

X_LOADS = (((0, 512),), ((0, 512),), ((0, 512),), ((0, 512),))
X_SCALAR = (((0, 168),), ((0, 256), (256, 320)), ((0, 256), (256, 368)), ((0, 256),))
X_VECTOR = (((168, 256), (256, 512)), ((320, 512),), ((368, 512),), ((256, 512),))
X_QUANT = (((0, 256), (256, 512)), ((0, 256), (256, 512)), ((0, 256), (256, 512)), ((0, 256), (256, 512)))
W_LOADS = ((0, 2), (2, 4), (4, 6), (6, 7), (7, 8))
W_QUANT = ((0, 2), (2, 4), (4, 6), (6, 7), (7, 8))
W_VECTOR_COLS = {}


def interleave_views(grouped, raw, cols):
    dst = grouped[:, cols, :].rearrange("p (c i) j -> p c j i", i=RUN)
    src = raw[:, :, cols].rearrange("p j (c i) -> p c j i", i=RUN)
    return dst, src


def tile_picked_merge_lin_none_sub_e_kernel(tc, xT, w, offs, out):
    nc = tc.nc

    def copy_scalar(grouped, raw, cols):
        dst, src = interleave_views(grouped, raw, cols)
        nc.scalar.activation(out=dst, in_=src, func=COPY)

    def copy_vector(grouped, raw, cols):
        dst, src = interleave_views(grouped, raw, cols)
        nc.vector.tensor_copy(out=dst, in_=src)

    with ExitStack() as ctx:
        keep = ctx.enter_context(tc.tile_pool(name="keep", bufs=1))
        psum = ctx.enter_context(tc.psum_pool(name="psum", bufs=1))

        units = [(d, a) for d in range(D) for a in range(LAST)] + [(d, LAST) for d in range(D)]
        loads = [(a, t0, t1) for a in range(PASSES) for t0, t1 in X_LOADS[a]]

        offsets = keep.tile([P, D * LIST_COLS], U16, name="offsets")
        x_raw = {
            (a, t0): keep.tile([P, PACK, t1 - t0], F32, name=f"x_raw{a}_{t0}", align_bytes=64) for a, t0, t1 in loads
        }
        x_bf = [keep.tile([P, T, PACK], BF16, name=f"x_bf{a}", align_bytes=64) for a in range(PASSES)]
        x_words = [keep.tile([P, T], U32, name=f"x_words{a}", align_bytes=64) for a in range(PASSES)]
        x_scales = keep.tile([P, T], U8, name="x_scales", align_bytes=64)
        w_raw = {
            i0: keep.tile([P, i1 - i0, PACK, N], F32, name=f"w_raw{i0}", tag=f"w_raw{i0}", align_bytes=64)
            for i0, i1 in W_LOADS
        }
        g_words = {
            (d, a): keep.tile([P, V], U32, name=f"g_words{d}_{a}", align_bytes=64) for d, a in units if a < LAST
        }
        g_scales = keep.tile([P, D, V], U8, name="g_scales", tag="w_raw0", align_bytes=64)
        g_words[0, LAST] = keep.tile([P, V], U32, name="g_words_last0", tag="w_raw2", align_bytes=64)
        g_words[1, LAST] = keep.tile([P, V], U32, name="g_words_last1", tag="w_raw4", align_bytes=64)
        w_bf = keep.tile([P, len(units), N, PACK], BF16, name="w_bf", align_bytes=64)
        w_words = keep.tile([P, len(units), N], U32, name="w_words", align_bytes=64)
        w_scales = keep.tile([P, len(units), N], U8, name="w_scales", align_bytes=64)
        warm_in = keep.tile([P, 2], F32, name="warm_in")
        warm_out = keep.tile([P, 2], BF16, name="warm_out")
        result = keep.tile([N, V], F32, name="result")
        acc = psum.tile([N, V], F32, name="acc")

        w_passes = w.rearrange("d (a p j) n -> p (d a) (j n)", p=P, j=PACK)

        for a, t0, t1 in loads:
            rows = xT[a * K_PASS : (a + 1) * K_PASS, t0:t1]
            nc.sync.dma_start(out=x_raw[a, t0][:], in_=rows.rearrange("(p j) t -> p j t", j=PACK))
            if (a, t0) == (0, 0):
                nc.sync.dma_start(offsets[:], offs)
        for i0, i1 in W_LOADS:
            first = units[i0][0] * PASSES + units[i0][1]
            final = units[i1 - 1][0] * PASSES + units[i1 - 1][1]
            step = max(final - first, 1) // max(i1 - i0 - 1, 1)
            nc.sync.dma_start(
                out=w_raw[i0][:].rearrange("p i j n -> p i (j n)"),
                in_=w_passes[:, first : final + 1 : step, :],
            )

        nc.vector.memset(warm_in[:], 0.0)
        nc.scalar.activation(out=warm_out[:], in_=warm_in[:], func=COPY)
        nc.gpsimd.memset(x_scales[:], 0)

        def copy_x(copy, a, t0, t1):
            base = max(b for b, e in X_LOADS[a] if b <= t0)
            copy(x_bf[a][:, base:, :], x_raw[a, base], slice(t0 - base, t1 - base))

        def quantize_x(a, t0, t1):
            nc.vector.quantize_mx(
                out=x_words[a][:, t0:t1].bitcast(FP8X4),
                scales=x_scales[PACK * a :, t0:t1],
                in_=x_bf[a][:, t0:t1, :].rearrange("p t j -> p (t j)"),
            )

        def piece(d):
            return offsets[:, d * LIST_COLS : (d + 1) * LIST_COLS]

        def gather_words(d, a):
            nc.vector.tensor_copy(out=g_words[d, a][:], in_=x_words[a][:].indirect(piece(d)))

        def gather_scales(d):
            nc.vector.tensor_copy(out=g_scales[:, d, :], in_=x_scales[:].indirect(piece(d)))

        def weights(i0, i1):
            for i in range(i0, i1):
                cut = N - W_VECTOR_COLS.get(i, 0)
                if cut > 0:
                    copy_scalar(w_bf[:, i, :, :], w_raw[i0][:, i - i0, :, :], slice(0, cut))
                if cut < N:
                    copy_vector(w_bf[:, i, :, :], w_raw[i0][:, i - i0, :, :], slice(cut, N))
            nc.vector.quantize_mx(
                out=w_words[:, i0:i1, :].rearrange("p i n -> p (i n)").bitcast(FP8X4),
                scales=w_scales[:, i0:i1, :].rearrange("p i n -> p (i n)"),
                in_=w_bf[:, i0:i1, :, :].rearrange("p i n j -> p (i n j)"),
            )

        def multiply(i0, i1):
            for i in range(i0, i1):
                d, a = units[i]
                nc.tensor.matmul_mx(
                    out=acc[:],
                    lhsT=w_words[:, i, :].bitcast(FP8X4),
                    lhsT_scale=w_scales[:, i, :],
                    rhs=g_words[d, a][:].bitcast(FP8X4),
                    rhs_scale=g_scales[PACK * a :, d, :],
                    start=(i == 0),
                    stop=(i == len(units) - 1),
                )

        for a in range(PASSES):
            for t0, t1 in X_SCALAR[a]:
                copy_x(copy_scalar, a, t0, t1)
            for t0, t1 in X_VECTOR[a]:
                copy_x(copy_vector, a, t0, t1)
            for t0, t1 in X_QUANT[a]:
                quantize_x(a, t0, t1)
            if a < LAST:
                for d in range(D):
                    gather_words(d, a)

        weights(*W_QUANT[0])
        gather_scales(0)
        gather_scales(1)
        multiply(*W_QUANT[0])
        weights(*W_QUANT[1])
        gather_words(0, LAST)
        multiply(*W_QUANT[1])
        weights(*W_QUANT[2])
        gather_words(1, LAST)
        multiply(*W_QUANT[2])
        for group in W_QUANT[3:]:
            weights(*group)
            multiply(*group)

        nc.vector.tensor_copy(out=result[:], in_=acc[:])
        nc.sync.dma_start(out=out, in_=result[:])
